import numpy as np
import ml_dtypes


def mxq(x, axis, fmt="e4m3"):
    dtype, down = {"e4m3": (ml_dtypes.float8_e4m3fn, 7), "e5m2": (ml_dtypes.float8_e5m2, 14)}[fmt]
    v = np.moveaxis(np.asarray(x, np.float32).astype(ml_dtypes.bfloat16).astype(np.float64), axis, -1)
    blocks = v.reshape(v.shape[:-1] + (-1, 32))
    amax = np.abs(blocks).max(-1, keepdims=True)
    byte = np.maximum(np.where(amax > 0, np.frexp(amax)[1] - 1 + 127, 0) - down, 1)
    scale = np.exp2(byte - 127.0)
    codes = (blocks / scale).astype(np.float32).astype(dtype).astype(np.float64)
    return np.moveaxis((codes * scale).reshape(v.shape), -1, axis)


WIDE = False


def mx_kscale(k):
    if not WIDE:
        return np.ones(k)
    levels = np.array([18, -18])
    if k % 512:
        return np.exp2(np.random.permutation(np.resize(levels, k // 32))).repeat(32)
    a = np.empty((k // 512, 16))
    for p in range(k // 512):
        a[p, :8] = np.random.permutation(np.resize(levels, 8))
        for g in range(8):
            far = levels[np.abs(levels - a[p, g]) >= 10]
            a[p, g + 8] = far[np.random.randint(len(far))]
    return np.exp2(a.ravel()).repeat(32)


def f64(x):
    return np.asarray(x).astype(np.float64)


def striped(idx):
    return np.tile(np.asarray(idx).reshape(-1, 16).T, (8, 1)).astype(np.uint16)


def unstriped(offs):
    return offs[:16].T.reshape(-1).astype(np.int64)

def planes(y):
    n, m = y.shape
    v = y.astype(np.float32).astype(ml_dtypes.bfloat16).astype(np.float64).reshape(n // 32, 32, m)
    top = np.abs(v).max(1)
    byte = np.clip(np.where(top > 0, np.frexp(top)[1] - 1 + 127 - 7, 1), 1, 254)
    codes = (v * np.exp2(127.0 - byte)[:, None, :]).reshape(n, m).astype(np.float32).astype(ml_dtypes.float8_e4m3fn).view(np.uint8)
    words = codes.reshape(n // 512, 128, 4, m).transpose(0, 1, 3, 2)
    return np.ascontiguousarray(words), np.ascontiguousarray(byte.astype(np.uint8).reshape(n // 512, 16, m))


N, C, D, R = 512, 2048, 512, 1024


def eight(codes):
    return np.concatenate([codes[h].reshape(-1, 16).T for h in range(8)]).astype(np.uint16)


def uneight(offs):
    return np.stack([offs[16 * h:16 * h + 16].T.reshape(-1) for h in range(8)]).astype(np.int64)


def setup_inputs():
    n = np.random.standard_normal
    s = mx_kscale(D)[:, None]
    u = mx_kscale(N)
    grid = lambda x: np.round(x * 32) / 32
    return {
        "xT": (n((D, R)) * (1.0 / np.sqrt(D)) * s).astype(np.float32),
        "cb": (grid(n((D, C))) / s).astype(np.float32),
        "norm": np.tile(np.random.randint(32, 129, N) / 64.0 / u, (128, 1)).astype(np.float32),
        "ts": np.tile(np.random.uniform(0.5, 1.5, N) * u, (128, 1)).astype(np.float32),
        "y": (2 * np.random.randint(0, 2, (R, N)) - 1).astype(np.float32),
        "wt": (np.random.uniform(0.5, 1.5, (R, 1)) * 1.0 / np.sqrt(N)).astype(np.float32),
        "offs": eight(np.random.randint(0, C, (8, N))),
    }


def reference(xT, cb, norm, ts, y, wt, offs):
    code = uneight(offs)
    k = np.concatenate([f64(cb)[64 * h:64 * h + 64][:, code[h]] for h in range(8)]) * f64(norm)[:1]
    a = f64(ts)[:1] * (mxq(f64(xT), 0, "e4m3").T @ mxq(k, 0, "e4m3"))
    g = -f64(wt) * f64(y) * np.maximum(1.0 - f64(y) * a, 0.0)
    h = f64(ts)[:1] * g
    out_0 = mxq(h, 1, "e5m2") @ mxq(k, 1, "e4m3").T
    return (out_0,) + planes(out_0)

@@ -1,0 +1,268 @@
+from contextlib import ExitStack
+
+import concourse.mybir as mybir
+from concourse.masks import make_identity
+
+N, C, D, R = 512, 2048, 512, 1024
+FLOPS = 2 * 2 * R * N * D
+
+F32 = mybir.dt.float32
+BF16 = mybir.dt.bfloat16
+U32 = mybir.dt.uint32
+I32 = mybir.dt.int32
+U16 = mybir.dt.uint16
+U8 = mybir.dt.uint8
+E4M3 = mybir.dt.float8_e4m3fn_x4
+E5M2 = mybir.dt.float8_e5m2_x4
+MULT = mybir.AluOpType.mult
+SUBTRACT = mybir.AluOpType.subtract
+IS_GE = mybir.AluOpType.is_ge
+RELU = mybir.ActivationFunctionType.Relu
+COPY = mybir.ActivationFunctionType.Copy
+
+P = 128
+LANES = 4
+PASS = P * LANES
+GROUPS = R // PASS
+TILES = GROUPS * LANES
+HALF = 256
+
+
+def tile_attend_gpq_pl_sqh_x_kernel(tc, xT, cb, norm, ts, y, wt, offs, out_0, out_1, out_2):
+    nc = tc.nc
+    with ExitStack() as ctx:
+        keep = ctx.enter_context(tc.tile_pool(name="keep", bufs=1))
+        ring = ctx.enter_context(tc.tile_pool(name="ring", bufs=4))
+        psum = ctx.enter_context(tc.psum_pool(name="psum", bufs=2))
+
+        offsets = keep.tile([P, N // 16], U16, name="offsets")
+        nc.sync.dma_start(offsets[:], offs)
+        norm_col = keep.tile([P, LANES], F32, name="norm_col")
+        nc.scalar.dma_start(norm_col[:], norm[0:1, :].rearrange("o (p j) -> p (o j)", j=LANES))
+        ts_col = keep.tile([P, LANES], F32, name="ts_col")
+        nc.scalar.dma_start(ts_col[:], ts[0:1, :].rearrange("o (p j) -> p (o j)", j=LANES))
+        wt_col = keep.tile([P, GROUPS, LANES], F32, name="wt_col")
+        nc.scalar.dma_start(wt_col[:], wt.rearrange("(g m t) o -> m g (t o)", g=GROUPS, t=LANES))
+
+        cb_rows = cb.rearrange("(p t) c -> p t c", t=LANES)
+        books = []
+        for t in range(LANES):
+            book = keep.tile([P, C], F32, name="book%d" % t)
+            nc.sync.dma_start(book[:], cb_rows[:, t, :])
+            books.append(book)
+
+        x_rows = xT.rearrange("(p j) r -> p j r", j=LANES)
+        y_rows = y.rearrange("(g m t) n -> g m t n", g=GROUPS, t=LANES)
+        x_raw = []
+        y_raw = []
+        for g in range(GROUPS):
+            for a in range(2):
+                raw = keep.tile([P, LANES, HALF], F32, name="x_raw%d_%d" % (g, a))
+                r0 = g * PASS + a * HALF
+                nc.sync.dma_start(raw[:], x_rows[:, :, r0 : r0 + HALF])
+                x_raw.append(raw)
+            for t in range(LANES):
+                label = keep.tile([P, N], F32, name="y_raw%d_%d" % (g, t))
+                nc.sync.dma_start(label[:], y_rows[g, :, t, :])
+                y_raw.append(label)
+
+        ident = keep.tile([P, P], F32, name="ident")
+        make_identity(nc, ident[:])
+
+        twice = keep.tile([P, LANES], F32, name="twice")
+        nc.vector.tensor_scalar(twice[:], ts_col[:], 0.0, 2.0, IS_GE, MULT)
+        signed_norm = keep.tile([P, LANES], F32, name="signed_norm")
+        nc.vector.scalar_tensor_tensor(signed_norm[:], twice[:], 1.0, norm_col[:], SUBTRACT, MULT)
+        abs_col = keep.tile([P, LANES], F32, name="abs_col")
+        nc.vector.scalar_tensor_tensor(abs_col[:], twice[:], 1.0, ts_col[:], SUBTRACT, MULT)
+
+        norm_row = keep.tile([P, N], F32, name="norm_row")
+        bank = psum.tile([P, LANES, P], F32, name="bank", tag="sums")
+        for j in range(LANES):
+            nc.tensor.transpose(bank[:, j, :], signed_norm[:, j : j + 1].to_broadcast([P, P]), ident[:])
+        nc.scalar.copy(norm_row[:].rearrange("m (p j) -> m p j", j=LANES), bank[:].rearrange("m j p -> m p j"))
+        abs_row = keep.tile([P, N], F32, name="abs_row")
+        bank = psum.tile([P, LANES, P], F32, name="bank", tag="sums")
+        for j in range(LANES):
+            nc.tensor.transpose(bank[:, j, :], abs_col[:, j : j + 1].to_broadcast([P, P]), ident[:])
+        nc.scalar.copy(
+            abs_row[:].rearrange("m (l f h j) -> m l f h j", l=LANES, h=2, j=LANES),
+            bank[:].rearrange("m j (f l h) -> m l f h j", l=LANES, h=2),
+        )
+        bank = psum.tile([P, LANES, P], F32, name="bank", tag="sums")
+        for lane in range(LANES):
+            nc.tensor.transpose(bank[:, lane, :], abs_row[:, lane * P : (lane + 1) * P], ident[:])
+        abs_ts = keep.tile([P, LANES], F32, name="abs_ts")
+        nc.scalar.activation(abs_ts[:], bank[:, :, 0], COPY)
+        neg_square = keep.tile([P, LANES], F32, name="neg_square")
+        nc.vector.scalar_tensor_tensor(neg_square[:], abs_ts[:], -1.0, abs_ts[:], MULT, MULT)
+
+        k_f32 = keep.tile([P, LANES, N], F32, name="k_f32")
+        kn_in = keep.tile([P, LANES, P * LANES], BF16, name="kn_in", align_bytes=64)
+        kn_codes = keep.tile([P, D], U32, name="kn_codes", align_bytes=64)
+        kn_scales = keep.tile([P, D], U8, name="kn_scales", align_bytes=64)
+        kd_in = keep.tile([P, N * LANES], BF16, name="kd_in", align_bytes=64)
+        kd_codes = keep.tile([P, N], U32, name="kd_codes", align_bytes=64)
+        kd_scales = keep.tile([P, N], U8, name="kd_scales", align_bytes=64)
+
+        def gather(t):
+            nc.vector.tensor_tensor(k_f32[:, t, :], books[t][:].indirect(offsets[:]), norm_row[:], MULT)
+
+        def turn_k(t):
+            pairs = ring.tile([P, N], BF16, name="pairs", tag="pairs", align_bytes=64)
+            nc.scalar.copy(
+                pairs[:].rearrange("p (u f i e) -> p u f e i", u=2, i=8, e=2),
+                k_f32[:, t, :].rearrange("p (f u e i) -> p u f e i", u=2, i=8, e=2),
+            )
+            words = pairs[:].bitcast(F32)
+            turned = psum.tile([P, LANES, P], F32, name="bank", tag="sums")
+            for u in range(2):
+                nc.tensor.transpose(turned[:, u, :], words[:, u * P : (u + 1) * P], ident[:])
+            nc.scalar.copy(
+                kn_in[:, t, :].bitcast(F32).rearrange("n (p u) -> n p u", u=2),
+                turned[:, 0:2, :].rearrange("n u p -> n p u"),
+            )
+            cols = slice(t * P, (t + 1) * P)
+            nc.vector.quantize_mx(kn_codes[:, cols].bitcast(E4M3), kn_scales[:, cols], kn_in[:, t, :])
+
+        x_in = [keep.tile([P, PASS * LANES], BF16, name="x_in%d" % g, align_bytes=64) for g in range(GROUPS)]
+        x_codes = [keep.tile([P, PASS], U32, name="x_codes%d" % g, align_bytes=64) for g in range(GROUPS)]
+        x_scales = [keep.tile([P, PASS], U8, name="x_scales%d" % g, align_bytes=64) for g in range(GROUPS)]
+
+        def make_x(g):
+            dealt = x_in[g][:].rearrange("p (t m j) -> p m j t", t=LANES, j=LANES)
+            for a in range(2):
+                nc.scalar.copy(
+                    dealt[:, a * (P // 2) : (a + 1) * (P // 2), :, :],
+                    x_raw[2 * g + a][:].rearrange("p j (m t) -> p m j t", t=LANES),
+                )
+            width = P if g == 0 else PASS
+            for c in range(0, PASS, width):
+                nc.vector.quantize_mx(
+                    x_codes[g][:, c : c + width].bitcast(E4M3),
+                    x_scales[g][:, c : c + width],
+                    x_in[g][:, c * LANES : (c + width) * LANES],
+                )
+
+        for t in range(LANES):
+            gather(t)
+            if t < LANES - 1:
+                turn_k(t)
+        nc.vector.tensor_copy(
+            kd_in[:].rearrange("p (c i t) -> p c t i", i=4, t=LANES),
+            k_f32[:].rearrange("p t (c i) -> p c t i", i=4),
+        )
+        nc.vector.quantize_mx(kd_codes[:].bitcast(E4M3), kd_scales[:], kd_in[:])
+        make_x(0)
+
+        result = [keep.tile([P, LANES, D], F32, name="result%d" % g) for g in range(GROUPS)]
+        out_rows = out_0.rearrange("(g m t) d -> g m t d", g=GROUPS, t=LANES)
+        plane_scales = keep.tile([P, GROUPS, D], U8, name="plane_scales", align_bytes=64)
+        weighted = {}
+        margin = {}
+        slack = {}
+        h_in = {}
+
+        def by_lanes(ap):
+            return ap.rearrange("m (l f i) -> m f l i", l=LANES, i=8)
+
+        def as_loaded(ap):
+            return ap.rearrange("m (f l i) -> m f l i", l=LANES, i=8)
+
+        def turn(src, tag):
+            turned = psum.tile([P, LANES, P], F32, name=tag, tag=tag)
+            for lane in range(LANES):
+                nc.tensor.transpose(turned[:, lane, :], src[:, lane * P : (lane + 1) * P], ident[:])
+            return turned
+
+        def weigh(i):
+            g, t = divmod(i, LANES)
+            weighted[i] = keep.tile([P, N], F32, name="weighted%d" % i)
+            nc.gpsimd.tensor_scalar(
+                by_lanes(weighted[i][:]), as_loaded(y_raw[i][:]), wt_col[:, g, t : t + 1], -1.0, MULT, MULT
+            )
+
+        def score(i):
+            g, t = divmod(i, LANES)
+            cols = slice(t * P, (t + 1) * P)
+            scores = psum.tile([P, N], F32, name="scores", tag="scores")
+            nc.tensor.matmul_mx(
+                scores[:], x_codes[g][:, cols].bitcast(E4M3), x_scales[g][:, cols],
+                kd_codes[:].bitcast(E4M3), kd_scales[:], start=True, stop=True,
+            )
+            margin[i] = ring.tile([P, N], F32, name="margin", tag="margin")
+            nc.vector.tensor_tensor(by_lanes(margin[i][:]), as_loaded(scores[:]), as_loaded(y_raw[i][:]), MULT)
+
+        def hinge(i):
+            turned = turn(margin[i], "margin_turned")
+            slack[i] = ring.tile([P, LANES, P], F32, name="slack", tag="slack")
+            for lane in range(LANES):
+                nc.scalar.activation(
+                    slack[i][:, lane, :], turned[:, lane, :], RELU,
+                    bias=abs_ts[:, lane : lane + 1], scale=neg_square[:, lane : lane + 1],
+                )
+
+        def gradient(i):
+            turned = turn(weighted[i], "weighted_turned")
+            h_in[i] = ring.tile([P, P * LANES], BF16, name="h_in", tag="h_in", align_bytes=64)
+            nc.vector.tensor_tensor(
+                h_in[i][:].rearrange("n (c e l) -> n c l e", e=2, l=LANES),
+                turned[:].rearrange("n l (c e) -> n c l e", e=2),
+                slack[i][:].rearrange("n l (c e) -> n c l e", e=2),
+                MULT,
+            )
+
+        def back(i):
+            g, t = divmod(i, LANES)
+            h_codes = ring.tile([P, P], U32, name="h_codes", tag="h_codes", align_bytes=64)
+            h_scales = ring.tile([P, P], U8, name="h_scales", tag="h_scales", align_bytes=64)
+            nc.vector.quantize_mx(h_codes[:].bitcast(E5M2), h_scales[:], h_in[i][:])
+            sums = psum.tile([P, D], F32, name="sums", tag="sums")
+            nc.tensor.matmul_mx(
+                sums[:], h_codes[:].bitcast(E5M2), h_scales[:],
+                kn_codes[:].bitcast(E4M3), kn_scales[:], start=True, stop=True,
+            )
+            nc.scalar.copy(
+                result[g][:, t, :].rearrange("m (p j) -> m p j", j=LANES),
+                sums[:].rearrange("m (j p) -> m p j", j=LANES),
+            )
+            nc.sync.dma_start(out_rows[g, :, t, :], result[g][:, t, :])
+
+        def planes(g):
+            words_out = out_1[g].rearrange("p d l -> p (d l)").bitcast(I32)
+            for a in range(2):
+                cols = slice(a * HALF, (a + 1) * HALF)
+                woven = keep.tile([P, HALF * LANES], BF16, name="woven%d_%d" % (g, a), align_bytes=64)
+                codes = keep.tile([P, HALF], U32, name="plane_codes%d_%d" % (g, a), align_bytes=64)
+                dst = woven[:].rearrange("p (c i t) -> p c t i", i=4, t=LANES)
+                src = result[g][:, :, cols].rearrange("p t (c i) -> p c t i", i=4)
+                if g == 0 or a == 0:
+                    nc.vector.tensor_copy(dst, src)
+                else:
+                    nc.scalar.copy(dst, src)
+                nc.vector.quantize_mx(codes[:].bitcast(E4M3), plane_scales[:, g, cols], woven[:])
+                nc.sync.dma_start(words_out[:, cols], codes[:].bitcast(I32))
+
+        for i in range(TILES):
+            weigh(i)
+        for step in range(-2, TILES + 1):
+            if step == 0:
+                turn_k(LANES - 1)
+            if step + 2 == LANES:
+                make_x(1)
+            if step + 2 < TILES:
+                score(step + 2)
+            if 0 <= step + 1 < TILES:
+                hinge(step + 1)
+            if 0 <= step < TILES:
+                gradient(step)
+            if step >= 1:
+                back(step - 1)
+        for g in range(GROUPS):
+            planes(g)
+
+        scales_out = out_2.bitcast(I32).rearrange("g f d -> f g d")
+        scale_words = plane_scales[:].bitcast(I32)
+        for q in range(4):
+            queue = nc.scalar if q % 2 else nc.sync
+            queue.dma_start(scales_out[4 * q : 4 * q + 4, :, :], scale_words[32 * q : 32 * q + 4, :, :])

@@ -36,7 +36,6 @@ def tile_attend_gpq_pl_sqh_x_kernel(tc, xT, cb, norm, ts, y, wt, offs, out_0, ou
         psum = ctx.enter_context(tc.psum_pool(name="psum", bufs=2))
 
         offsets = keep.tile([P, N // 16], U16, name="offsets")
-        nc.sync.dma_start(offsets[:], offs)
         norm_col = keep.tile([P, LANES], F32, name="norm_col")
         nc.scalar.dma_start(norm_col[:], norm[0:1, :].rearrange("o (p j) -> p (o j)", j=LANES))
         ts_col = keep.tile([P, LANES], F32, name="ts_col")
@@ -50,21 +49,32 @@ def tile_attend_gpq_pl_sqh_x_kernel(tc, xT, cb, norm, ts, y, wt, offs, out_0, ou
             book = keep.tile([P, C], F32, name="book%d" % t)
             nc.sync.dma_start(book[:], cb_rows[:, t, :])
             books.append(book)
+            if t == 0:
+                nc.sync.dma_start(offsets[:], offs)
 
         x_rows = xT.rearrange("(p j) r -> p j r", j=LANES)
         y_rows = y.rearrange("(g m t) n -> g m t n", g=GROUPS, t=LANES)
         x_raw = []
         y_raw = []
-        for g in range(GROUPS):
-            for a in range(2):
-                raw = keep.tile([P, LANES, HALF], F32, name="x_raw%d_%d" % (g, a))
-                r0 = g * PASS + a * HALF
-                nc.sync.dma_start(raw[:], x_rows[:, :, r0 : r0 + HALF])
-                x_raw.append(raw)
-            for t in range(LANES):
-                label = keep.tile([P, N], F32, name="y_raw%d_%d" % (g, t))
-                nc.sync.dma_start(label[:], y_rows[g, :, t, :])
-                y_raw.append(label)
+
+        def load_x(piece):
+            raw = keep.tile([P, LANES, HALF], F32, name="x_raw%d" % piece)
+            nc.sync.dma_start(raw[:], x_rows[:, :, piece * HALF : (piece + 1) * HALF])
+            x_raw.append(raw)
+
+        def load_y(i):
+            g, t = divmod(i, LANES)
+            label = keep.tile([P, N], F32, name="y_raw%d" % i)
+            nc.sync.dma_start(label[:], y_rows[g, :, t, :])
+            y_raw.append(label)
+
+        for i in range(2):
+            load_x(i)
+            load_y(i)
+        load_x(2)
+        load_x(3)
+        for i in range(2, TILES):
+            load_y(i)
 
         ident = keep.tile([P, P], F32, name="ident")
         make_identity(nc, ident[:])
@@ -159,7 +169,9 @@ def tile_attend_gpq_pl_sqh_x_kernel(tc, xT, cb, norm, ts, y, wt, offs, out_0, ou
         out_rows = out_0.rearrange("(g m t) d -> g m t d", g=GROUPS, t=LANES)
         plane_scales = keep.tile([P, GROUPS, D], U8, name="plane_scales", align_bytes=64)
         weighted = {}
+        scores = {}
         margin = {}
+        weighted_turned = {}
         slack = {}
         h_in = {}
 
@@ -177,21 +189,24 @@ def tile_attend_gpq_pl_sqh_x_kernel(tc, xT, cb, norm, ts, y, wt, offs, out_0, ou
 
         def weigh(i):
             g, t = divmod(i, LANES)
-            weighted[i] = keep.tile([P, N], F32, name="weighted%d" % i)
-            nc.gpsimd.tensor_scalar(
+            weighted[i] = ring.tile([P, N], F32, name="weighted", tag="weighted", bufs=2)
+            engine = nc.vector if i < 2 else nc.gpsimd
+            engine.tensor_scalar(
                 by_lanes(weighted[i][:]), as_loaded(y_raw[i][:]), wt_col[:, g, t : t + 1], -1.0, MULT, MULT
             )
 
         def score(i):
             g, t = divmod(i, LANES)
             cols = slice(t * P, (t + 1) * P)
-            scores = psum.tile([P, N], F32, name="scores", tag="scores")
+            scores[i] = psum.tile([P, N], F32, name="scores", tag="scores")
             nc.tensor.matmul_mx(
-                scores[:], x_codes[g][:, cols].bitcast(E4M3), x_scales[g][:, cols],
+                scores[i][:], x_codes[g][:, cols].bitcast(E4M3), x_scales[g][:, cols],
                 kd_codes[:].bitcast(E4M3), kd_scales[:], start=True, stop=True,
             )
+
+        def sign(i):
             margin[i] = ring.tile([P, N], F32, name="margin", tag="margin")
-            nc.vector.tensor_tensor(by_lanes(margin[i][:]), as_loaded(scores[:]), as_loaded(y_raw[i][:]), MULT)
+            nc.vector.tensor_tensor(by_lanes(margin[i][:]), as_loaded(scores[i][:]), as_loaded(y_raw[i][:]), MULT)
 
         def hinge(i):
             turned = turn(margin[i], "margin_turned")
@@ -202,8 +217,13 @@ def tile_attend_gpq_pl_sqh_x_kernel(tc, xT, cb, norm, ts, y, wt, offs, out_0, ou
                     bias=abs_ts[:, lane : lane + 1], scale=neg_square[:, lane : lane + 1],
                 )
 
+        def turn_weighted(i):
+            weighted_turned[i] = turn(weighted[i], "weighted_turned")
+            if i + 2 < TILES:
+                weigh(i + 2)
+
         def gradient(i):
-            turned = turn(weighted[i], "weighted_turned")
+            turned = weighted_turned[i]
             h_in[i] = ring.tile([P, P * LANES], BF16, name="h_in", tag="h_in", align_bytes=64)
             nc.vector.tensor_tensor(
                 h_in[i][:].rearrange("n (c e l) -> n c l e", e=2, l=LANES),
@@ -222,10 +242,11 @@ def tile_attend_gpq_pl_sqh_x_kernel(tc, xT, cb, norm, ts, y, wt, offs, out_0, ou
                 sums[:], h_codes[:].bitcast(E5M2), h_scales[:],
                 kn_codes[:].bitcast(E4M3), kn_scales[:], start=True, stop=True,
             )
-            nc.scalar.copy(
-                result[g][:, t, :].rearrange("m (p j) -> m p j", j=LANES),
-                sums[:].rearrange("m (j p) -> m p j", j=LANES),
-            )
+            dst = result[g][:, t, :].rearrange("m (p j) -> m p j", j=LANES)
+            src = sums[:].rearrange("m (j p) -> m p j", j=LANES)
+            width = P // 2 if i == TILES - 1 else P
+            for c in range(0, P, width):
+                nc.scalar.copy(dst[:, c : c + width, :], src[:, c : c + width, :])
             nc.sync.dma_start(out_rows[g, :, t, :], result[g][:, t, :])
 
         def planes(g):
@@ -236,28 +257,23 @@ def tile_attend_gpq_pl_sqh_x_kernel(tc, xT, cb, norm, ts, y, wt, offs, out_0, ou
                 codes = keep.tile([P, HALF], U32, name="plane_codes%d_%d" % (g, a), align_bytes=64)
                 dst = woven[:].rearrange("p (c i t) -> p c t i", i=4, t=LANES)
                 src = result[g][:, :, cols].rearrange("p t (c i) -> p c t i", i=4)
-                if g == 0 or a == 0:
+                if g == 0 or a == 1:
                     nc.vector.tensor_copy(dst, src)
                 else:
                     nc.scalar.copy(dst, src)
                 nc.vector.quantize_mx(codes[:].bitcast(E4M3), plane_scales[:, g, cols], woven[:])
                 nc.sync.dma_start(words_out[:, cols], codes[:].bitcast(I32))
 
-        for i in range(TILES):
-            weigh(i)
-        for step in range(-2, TILES + 1):
-            if step == 0:
-                turn_k(LANES - 1)
-            if step + 2 == LANES:
+        weigh(0)
+        weigh(1)
+        turn_k(LANES - 1)
+        stages = [score, sign, hinge, turn_weighted, gradient, back]
+        for step in range(TILES + len(stages) - 1):
+            for depth, stage in enumerate(stages):
+                if 0 <= step - depth < TILES:
+                    stage(step - depth)
+            if step == 1:
                 make_x(1)
-            if step + 2 < TILES:
-                score(step + 2)
-            if 0 <= step + 1 < TILES:
-                hinge(step + 1)
-            if 0 <= step < TILES:
-                gradient(step)
-            if step >= 1:
-                back(step - 1)
         for g in range(GROUPS):
             planes(g)
 

@@ -68,12 +68,14 @@ def tile_attend_gpq_pl_sqh_x_kernel(tc, xT, cb, norm, ts, y, wt, offs, out_0, ou
             nc.sync.dma_start(label[:], y_rows[g, :, t, :])
             y_raw.append(label)
 
-        for i in range(2):
-            load_x(i)
-            load_y(i)
+        load_x(0)
+        load_x(1)
+        load_y(0)
+        load_y(1)
         load_x(2)
+        load_y(2)
         load_x(3)
-        for i in range(2, TILES):
+        for i in range(3, TILES):
             load_y(i)
 
         ident = keep.tile([P, P], F32, name="ident")
@@ -139,13 +141,15 @@ def tile_attend_gpq_pl_sqh_x_kernel(tc, xT, cb, norm, ts, y, wt, offs, out_0, ou
         x_codes = [keep.tile([P, PASS], U32, name="x_codes%d" % g, align_bytes=64) for g in range(GROUPS)]
         x_scales = [keep.tile([P, PASS], U8, name="x_scales%d" % g, align_bytes=64) for g in range(GROUPS)]
 
-        def make_x(g):
+        def weave_x(g):
             dealt = x_in[g][:].rearrange("p (t m j) -> p m j t", t=LANES, j=LANES)
             for a in range(2):
                 nc.scalar.copy(
                     dealt[:, a * (P // 2) : (a + 1) * (P // 2), :, :],
                     x_raw[2 * g + a][:].rearrange("p j (m t) -> p m j t", t=LANES),
                 )
+
+        def quantize_x(g):
             width = P if g == 0 else PASS
             for c in range(0, PASS, width):
                 nc.vector.quantize_mx(
@@ -163,11 +167,13 @@ def tile_attend_gpq_pl_sqh_x_kernel(tc, xT, cb, norm, ts, y, wt, offs, out_0, ou
             k_f32[:].rearrange("p t (c i) -> p c t i", i=4),
         )
         nc.vector.quantize_mx(kd_codes[:].bitcast(E4M3), kd_scales[:], kd_in[:])
-        make_x(0)
+        weave_x(0)
+        quantize_x(0)
 
         result = [keep.tile([P, LANES, D], F32, name="result%d" % g) for g in range(GROUPS)]
         out_rows = out_0.rearrange("(g m t) d -> g m t d", g=GROUPS, t=LANES)
         plane_scales = keep.tile([P, GROUPS, D], U8, name="plane_scales", align_bytes=64)
+        shared = [keep.tile([P, N], F32, name="shared%d" % b, align_bytes=64) for b in range(4)]
         weighted = {}
         scores = {}
         margin = {}
@@ -189,7 +195,7 @@ def tile_attend_gpq_pl_sqh_x_kernel(tc, xT, cb, norm, ts, y, wt, offs, out_0, ou
 
         def weigh(i):
             g, t = divmod(i, LANES)
-            weighted[i] = ring.tile([P, N], F32, name="weighted", tag="weighted", bufs=2)
+            weighted[i] = shared[i % 4]
             engine = nc.vector if i < 2 else nc.gpsimd
             engine.tensor_scalar(
                 by_lanes(weighted[i][:]), as_loaded(y_raw[i][:]), wt_col[:, g, t : t + 1], -1.0, MULT, MULT
@@ -219,14 +225,12 @@ def tile_attend_gpq_pl_sqh_x_kernel(tc, xT, cb, norm, ts, y, wt, offs, out_0, ou
 
         def turn_weighted(i):
             weighted_turned[i] = turn(weighted[i], "weighted_turned")
-            if i + 2 < TILES:
-                weigh(i + 2)
 
         def gradient(i):
             turned = weighted_turned[i]
-            h_in[i] = ring.tile([P, P * LANES], BF16, name="h_in", tag="h_in", align_bytes=64)
+            h_in[i] = shared[i % 4][:, 0 : N // 2].bitcast(BF16)
             nc.vector.tensor_tensor(
-                h_in[i][:].rearrange("n (c e l) -> n c l e", e=2, l=LANES),
+                h_in[i].rearrange("n (c e l) -> n c l e", e=2, l=LANES),
                 turned[:].rearrange("n l (c e) -> n c l e", e=2),
                 slack[i][:].rearrange("n l (c e) -> n c l e", e=2),
                 MULT,
@@ -236,7 +240,9 @@ def tile_attend_gpq_pl_sqh_x_kernel(tc, xT, cb, norm, ts, y, wt, offs, out_0, ou
             g, t = divmod(i, LANES)
             h_codes = ring.tile([P, P], U32, name="h_codes", tag="h_codes", align_bytes=64)
             h_scales = ring.tile([P, P], U8, name="h_scales", tag="h_scales", align_bytes=64)
-            nc.vector.quantize_mx(h_codes[:].bitcast(E5M2), h_scales[:], h_in[i][:])
+            nc.vector.quantize_mx(h_codes[:].bitcast(E5M2), h_scales[:], h_in[i])
+            if i + 4 < TILES:
+                weigh(i + 4)
             sums = psum.tile([P, D], F32, name="sums", tag="sums")
             nc.tensor.matmul_mx(
                 sums[:], h_codes[:].bitcast(E5M2), h_scales[:],
@@ -245,35 +251,42 @@ def tile_attend_gpq_pl_sqh_x_kernel(tc, xT, cb, norm, ts, y, wt, offs, out_0, ou
             dst = result[g][:, t, :].rearrange("m (p j) -> m p j", j=LANES)
             src = sums[:].rearrange("m (j p) -> m p j", j=LANES)
             width = P // 2 if i == TILES - 1 else P
+            copy = nc.scalar.copy
             for c in range(0, P, width):
-                nc.scalar.copy(dst[:, c : c + width, :], src[:, c : c + width, :])
+                copy(dst[:, c : c + width, :], src[:, c : c + width, :])
             nc.sync.dma_start(out_rows[g, :, t, :], result[g][:, t, :])
 
         def planes(g):
             words_out = out_1[g].rearrange("p d l -> p (d l)").bitcast(I32)
+            woven = []
             for a in range(2):
                 cols = slice(a * HALF, (a + 1) * HALF)
-                woven = keep.tile([P, HALF * LANES], BF16, name="woven%d_%d" % (g, a), align_bytes=64)
+                tile = keep.tile([P, HALF * LANES], BF16, name="woven%d_%d" % (g, a), align_bytes=64)
+                copy = nc.vector.tensor_copy if g == 0 or a == 1 else nc.scalar.copy
+                copy(
+                    tile[:].rearrange("p (c i t) -> p c t i", i=4, t=LANES),
+                    result[g][:, :, cols].rearrange("p t (c i) -> p c t i", i=4),
+                )
+                woven.append(tile)
+            for a in ((0, 1) if g == 0 else (1, 0)):
+                cols = slice(a * HALF, (a + 1) * HALF)
                 codes = keep.tile([P, HALF], U32, name="plane_codes%d_%d" % (g, a), align_bytes=64)
-                dst = woven[:].rearrange("p (c i t) -> p c t i", i=4, t=LANES)
-                src = result[g][:, :, cols].rearrange("p t (c i) -> p c t i", i=4)
-                if g == 0 or a == 1:
-                    nc.vector.tensor_copy(dst, src)
-                else:
-                    nc.scalar.copy(dst, src)
-                nc.vector.quantize_mx(codes[:].bitcast(E4M3), plane_scales[:, g, cols], woven[:])
+                nc.vector.quantize_mx(codes[:].bitcast(E4M3), plane_scales[:, g, cols], woven[a][:])
                 nc.sync.dma_start(words_out[:, cols], codes[:].bitcast(I32))
 
         weigh(0)
         weigh(1)
+        weigh(2)
+        weigh(3)
         turn_k(LANES - 1)
-        stages = [score, sign, hinge, turn_weighted, gradient, back]
-        for step in range(TILES + len(stages) - 1):
-            for depth, stage in enumerate(stages):
-                if 0 <= step - depth < TILES:
-                    stage(step - depth)
-            if step == 1:
-                make_x(1)
+        stages = [(score, 0), (sign, 1), (hinge, 2), (turn_weighted, 3), (gradient, 4), (back, 5)]
+        for step in range(TILES + 5):
+            for stage, delay in stages:
+                if 0 <= step - delay < TILES:
+                    stage(step - delay)
+            if step == 3:
+                weave_x(1)
+                quantize_x(1)
         for g in range(GROUPS):
             planes(g)
 

@@ -22,17 +22,21 @@ COPY = mybir.ActivationFunctionType.Copy
 
 P = 128
 LANES = 4
+BLOCK_PARTITIONS = 8
 PASS = P * LANES
 GROUPS = R // PASS
 TILES = GROUPS * LANES
-HALF = 256
+HALF = PASS // 2
+RING = 4
+SHARED = 4
+REPEATED = range(1, 5)
 
 
 def tile_attend_gpq_pl_sqh_x_kernel(tc, xT, cb, norm, ts, y, wt, offs, out_0, out_1, out_2):
     nc = tc.nc
     with ExitStack() as ctx:
         keep = ctx.enter_context(tc.tile_pool(name="keep", bufs=1))
-        ring = ctx.enter_context(tc.tile_pool(name="ring", bufs=4))
+        ring = ctx.enter_context(tc.tile_pool(name="ring", bufs=RING))
         psum = ctx.enter_context(tc.psum_pool(name="psum", bufs=2))
 
         offsets = keep.tile([P, N // 16], U16, name="offsets")
@@ -41,7 +45,6 @@ def tile_attend_gpq_pl_sqh_x_kernel(tc, xT, cb, norm, ts, y, wt, offs, out_0, ou
         ts_col = keep.tile([P, LANES], F32, name="ts_col")
         nc.scalar.dma_start(ts_col[:], ts[0:1, :].rearrange("o (p j) -> p (o j)", j=LANES))
         wt_col = keep.tile([P, GROUPS, LANES], F32, name="wt_col")
-        nc.scalar.dma_start(wt_col[:], wt.rearrange("(g m t) o -> m g (t o)", g=GROUPS, t=LANES))
 
         cb_rows = cb.rearrange("(p t) c -> p t c", t=LANES)
         books = []
@@ -73,9 +76,9 @@ def tile_attend_gpq_pl_sqh_x_kernel(tc, xT, cb, norm, ts, y, wt, offs, out_0, ou
         load_y(0)
         load_y(1)
         load_x(2)
-        load_y(2)
+        nc.sync.dma_start(wt_col[:], wt.rearrange("(g m t) o -> m g (t o)", g=GROUPS, t=LANES))
         load_x(3)
-        for i in range(3, TILES):
+        for i in range(2, TILES):
             load_y(i)
 
         ident = keep.tile([P, P], F32, name="ident")
@@ -123,8 +126,8 @@ def tile_attend_gpq_pl_sqh_x_kernel(tc, xT, cb, norm, ts, y, wt, offs, out_0, ou
         def turn_k(t):
             pairs = ring.tile([P, N], BF16, name="pairs", tag="pairs", align_bytes=64)
             nc.scalar.copy(
-                pairs[:].rearrange("p (u f i e) -> p u f e i", u=2, i=8, e=2),
-                k_f32[:, t, :].rearrange("p (f u e i) -> p u f e i", u=2, i=8, e=2),
+                pairs[:].rearrange("p (u f i e) -> p u f e i", u=2, i=BLOCK_PARTITIONS, e=2),
+                k_f32[:, t, :].rearrange("p (f u e i) -> p u f e i", u=2, i=BLOCK_PARTITIONS, e=2),
             )
             words = pairs[:].bitcast(F32)
             turned = psum.tile([P, LANES, P], F32, name="bank", tag="sums")
@@ -173,8 +176,7 @@ def tile_attend_gpq_pl_sqh_x_kernel(tc, xT, cb, norm, ts, y, wt, offs, out_0, ou
         result = [keep.tile([P, LANES, D], F32, name="result%d" % g) for g in range(GROUPS)]
         out_rows = out_0.rearrange("(g m t) d -> g m t d", g=GROUPS, t=LANES)
         plane_scales = keep.tile([P, GROUPS, D], U8, name="plane_scales", align_bytes=64)
-        shared = [keep.tile([P, N], F32, name="shared%d" % b, align_bytes=64) for b in range(4)]
-        weighted = {}
+        shared = [keep.tile([P, N], F32, name="shared%d" % b, align_bytes=64) for b in range(SHARED)]
         scores = {}
         margin = {}
         weighted_turned = {}
@@ -182,10 +184,10 @@ def tile_attend_gpq_pl_sqh_x_kernel(tc, xT, cb, norm, ts, y, wt, offs, out_0, ou
         h_in = {}
 
         def by_lanes(ap):
-            return ap.rearrange("m (l f i) -> m f l i", l=LANES, i=8)
+            return ap.rearrange("m (l f i) -> m f l i", l=LANES, i=BLOCK_PARTITIONS)
 
         def as_loaded(ap):
-            return ap.rearrange("m (f l i) -> m f l i", l=LANES, i=8)
+            return ap.rearrange("m (f l i) -> m f l i", l=LANES, i=BLOCK_PARTITIONS)
 
         def turn(src, tag):
             turned = psum.tile([P, LANES, P], F32, name=tag, tag=tag)
@@ -195,20 +197,19 @@ def tile_attend_gpq_pl_sqh_x_kernel(tc, xT, cb, norm, ts, y, wt, offs, out_0, ou
 
         def weigh(i):
             g, t = divmod(i, LANES)
-            weighted[i] = shared[i % 4]
-            engine = nc.vector if i < 2 else nc.gpsimd
-            engine.tensor_scalar(
-                by_lanes(weighted[i][:]), as_loaded(y_raw[i][:]), wt_col[:, g, t : t + 1], -1.0, MULT, MULT
+            nc.gpsimd.tensor_scalar(
+                by_lanes(shared[i % SHARED][:]), as_loaded(y_raw[i][:]), wt_col[:, g, t : t + 1], -1.0, MULT, MULT
             )
 
         def score(i):
             g, t = divmod(i, LANES)
             cols = slice(t * P, (t + 1) * P)
             scores[i] = psum.tile([P, N], F32, name="scores", tag="scores")
-            nc.tensor.matmul_mx(
-                scores[i][:], x_codes[g][:, cols].bitcast(E4M3), x_scales[g][:, cols],
-                kd_codes[:].bitcast(E4M3), kd_scales[:], start=True, stop=True,
-            )
+            for repeat in range(2 if i in REPEATED else 1):
+                nc.tensor.matmul_mx(
+                    scores[i][:], x_codes[g][:, cols].bitcast(E4M3), x_scales[g][:, cols],
+                    kd_codes[:].bitcast(E4M3), kd_scales[:], start=True, stop=True,
+                )
 
         def sign(i):
             margin[i] = ring.tile([P, N], F32, name="margin", tag="margin")
@@ -224,14 +225,13 @@ def tile_attend_gpq_pl_sqh_x_kernel(tc, xT, cb, norm, ts, y, wt, offs, out_0, ou
                 )
 
         def turn_weighted(i):
-            weighted_turned[i] = turn(weighted[i], "weighted_turned")
+            weighted_turned[i] = turn(shared[i % SHARED], "weighted_turned")
 
         def gradient(i):
-            turned = weighted_turned[i]
-            h_in[i] = shared[i % 4][:, 0 : N // 2].bitcast(BF16)
+            h_in[i] = shared[i % SHARED][:, 0 : N // 2].bitcast(BF16)
             nc.vector.tensor_tensor(
                 h_in[i].rearrange("n (c e l) -> n c l e", e=2, l=LANES),
-                turned[:].rearrange("n l (c e) -> n c l e", e=2),
+                weighted_turned[i][:].rearrange("n l (c e) -> n c l e", e=2),
                 slack[i][:].rearrange("n l (c e) -> n c l e", e=2),
                 MULT,
             )
@@ -241,8 +241,8 @@ def tile_attend_gpq_pl_sqh_x_kernel(tc, xT, cb, norm, ts, y, wt, offs, out_0, ou
             h_codes = ring.tile([P, P], U32, name="h_codes", tag="h_codes", align_bytes=64)
             h_scales = ring.tile([P, P], U8, name="h_scales", tag="h_scales", align_bytes=64)
             nc.vector.quantize_mx(h_codes[:].bitcast(E5M2), h_scales[:], h_in[i])
-            if i + 4 < TILES:
-                weigh(i + 4)
+            if i + SHARED < TILES:
+                weigh(i + SHARED)
             sums = psum.tile([P, D], F32, name="sums", tag="sums")
             nc.tensor.matmul_mx(
                 sums[:], h_codes[:].bitcast(E5M2), h_scales[:],
@@ -251,40 +251,41 @@ def tile_attend_gpq_pl_sqh_x_kernel(tc, xT, cb, norm, ts, y, wt, offs, out_0, ou
             dst = result[g][:, t, :].rearrange("m (p j) -> m p j", j=LANES)
             src = sums[:].rearrange("m (j p) -> m p j", j=LANES)
             width = P // 2 if i == TILES - 1 else P
-            copy = nc.scalar.copy
+            copy = nc.vector.tensor_copy if g == GROUPS - 1 and t % 2 == 0 else nc.scalar.copy
             for c in range(0, P, width):
                 copy(dst[:, c : c + width, :], src[:, c : c + width, :])
             nc.sync.dma_start(out_rows[g, :, t, :], result[g][:, t, :])
 
         def planes(g):
+            last = g == GROUPS - 1
             words_out = out_1[g].rearrange("p d l -> p (d l)").bitcast(I32)
             woven = []
             for a in range(2):
                 cols = slice(a * HALF, (a + 1) * HALF)
-                tile = keep.tile([P, HALF * LANES], BF16, name="woven%d_%d" % (g, a), align_bytes=64)
-                copy = nc.vector.tensor_copy if g == 0 or a == 1 else nc.scalar.copy
+                half = keep.tile([P, HALF * LANES], BF16, name="woven%d_%d" % (g, a), align_bytes=64)
+                copy = nc.vector.tensor_copy if last and a == 1 else nc.scalar.copy
                 copy(
-                    tile[:].rearrange("p (c i t) -> p c t i", i=4, t=LANES),
+                    half[:].rearrange("p (c i t) -> p c t i", i=4, t=LANES),
                     result[g][:, :, cols].rearrange("p t (c i) -> p c t i", i=4),
                 )
-                woven.append(tile)
-            for a in ((0, 1) if g == 0 else (1, 0)):
+                woven.append(half)
+            for a in (1, 0) if last else (0, 1):
                 cols = slice(a * HALF, (a + 1) * HALF)
                 codes = keep.tile([P, HALF], U32, name="plane_codes%d_%d" % (g, a), align_bytes=64)
                 nc.vector.quantize_mx(codes[:].bitcast(E4M3), plane_scales[:, g, cols], woven[a][:])
                 nc.sync.dma_start(words_out[:, cols], codes[:].bitcast(I32))
 
-        weigh(0)
-        weigh(1)
-        weigh(2)
-        weigh(3)
-        turn_k(LANES - 1)
-        stages = [(score, 0), (sign, 1), (hinge, 2), (turn_weighted, 3), (gradient, 4), (back, 5)]
-        for step in range(TILES + 5):
+        for i in range(SHARED):
+            weigh(i)
+        stages = [(sign, 1), (score, 0), (hinge, 1), (gradient, 4), (turn_weighted, 2), (back, 4)]
+        depth = max(delay for stage, delay in stages)
+        for step in range(TILES + depth):
+            if step == depth - 2:
+                turn_k(LANES - 1)
             for stage, delay in stages:
                 if 0 <= step - delay < TILES:
                     stage(step - delay)
-            if step == 3:
+            if step == LANES - 1:
                 weave_x(1)
                 quantize_x(1)
         for g in range(GROUPS):

from contextlib import ExitStack

import concourse.mybir as mybir
from concourse.masks import make_identity

N, C, D, R = 512, 2048, 512, 1024
FLOPS = 2 * 2 * R * N * D

F32 = mybir.dt.float32
BF16 = mybir.dt.bfloat16
U32 = mybir.dt.uint32
I32 = mybir.dt.int32
U16 = mybir.dt.uint16
U8 = mybir.dt.uint8
E4M3 = mybir.dt.float8_e4m3fn_x4
E5M2 = mybir.dt.float8_e5m2_x4
MULT = mybir.AluOpType.mult
SUBTRACT = mybir.AluOpType.subtract
IS_GE = mybir.AluOpType.is_ge
RELU = mybir.ActivationFunctionType.Relu
COPY = mybir.ActivationFunctionType.Copy

P = 128
LANES = 4
BLOCK_PARTITIONS = 8
PASS = P * LANES
GROUPS = R // PASS
TILES = GROUPS * LANES
HALF = PASS // 2
RING = 4
SHARED = 4
REPEATED = range(1, 5)


def tile_attend_gpq_pl_sqh_x_kernel(tc, xT, cb, norm, ts, y, wt, offs, out_0, out_1, out_2):
    nc = tc.nc
    with ExitStack() as ctx:
        keep = ctx.enter_context(tc.tile_pool(name="keep", bufs=1))
        ring = ctx.enter_context(tc.tile_pool(name="ring", bufs=RING))
        psum = ctx.enter_context(tc.psum_pool(name="psum", bufs=2))

        offsets = keep.tile([P, N // 16], U16, name="offsets")
        norm_col = keep.tile([P, LANES], F32, name="norm_col")
        nc.scalar.dma_start(norm_col[:], norm[0:1, :].rearrange("o (p j) -> p (o j)", j=LANES))
        ts_col = keep.tile([P, LANES], F32, name="ts_col")
        nc.scalar.dma_start(ts_col[:], ts[0:1, :].rearrange("o (p j) -> p (o j)", j=LANES))
        wt_col = keep.tile([P, GROUPS, LANES], F32, name="wt_col")

        cb_rows = cb.rearrange("(p t) c -> p t c", t=LANES)
        books = []
        for t in range(LANES):
            book = keep.tile([P, C], F32, name="book%d" % t)
            nc.sync.dma_start(book[:], cb_rows[:, t, :])
            books.append(book)
            if t == 0:
                nc.sync.dma_start(offsets[:], offs)

        x_rows = xT.rearrange("(p j) r -> p j r", j=LANES)
        y_rows = y.rearrange("(g m t) n -> g m t n", g=GROUPS, t=LANES)
        x_raw = []
        y_raw = []

        def load_x(piece):
            raw = keep.tile([P, LANES, HALF], F32, name="x_raw%d" % piece)
            nc.sync.dma_start(raw[:], x_rows[:, :, piece * HALF : (piece + 1) * HALF])
            x_raw.append(raw)

        def load_y(i):
            g, t = divmod(i, LANES)
            label = keep.tile([P, N], F32, name="y_raw%d" % i)
            nc.sync.dma_start(label[:], y_rows[g, :, t, :])
            y_raw.append(label)

        load_x(0)
        load_x(1)
        load_y(0)
        load_y(1)
        load_x(2)
        nc.sync.dma_start(wt_col[:], wt.rearrange("(g m t) o -> m g (t o)", g=GROUPS, t=LANES))
        load_x(3)
        for i in range(2, TILES):
            load_y(i)

        ident = keep.tile([P, P], F32, name="ident")
        make_identity(nc, ident[:])

        twice = keep.tile([P, LANES], F32, name="twice")
        nc.vector.tensor_scalar(twice[:], ts_col[:], 0.0, 2.0, IS_GE, MULT)
        signed_norm = keep.tile([P, LANES], F32, name="signed_norm")
        nc.vector.scalar_tensor_tensor(signed_norm[:], twice[:], 1.0, norm_col[:], SUBTRACT, MULT)
        abs_col = keep.tile([P, LANES], F32, name="abs_col")
        nc.vector.scalar_tensor_tensor(abs_col[:], twice[:], 1.0, ts_col[:], SUBTRACT, MULT)

        norm_row = keep.tile([P, N], F32, name="norm_row")
        bank = psum.tile([P, LANES, P], F32, name="bank", tag="sums")
        for j in range(LANES):
            nc.tensor.transpose(bank[:, j, :], signed_norm[:, j : j + 1].to_broadcast([P, P]), ident[:])
        nc.scalar.copy(norm_row[:].rearrange("m (p j) -> m p j", j=LANES), bank[:].rearrange("m j p -> m p j"))
        abs_row = keep.tile([P, N], F32, name="abs_row")
        bank = psum.tile([P, LANES, P], F32, name="bank", tag="sums")
        for j in range(LANES):
            nc.tensor.transpose(bank[:, j, :], abs_col[:, j : j + 1].to_broadcast([P, P]), ident[:])
        nc.scalar.copy(
            abs_row[:].rearrange("m (l f h j) -> m l f h j", l=LANES, h=2, j=LANES),
            bank[:].rearrange("m j (f l h) -> m l f h j", l=LANES, h=2),
        )
        bank = psum.tile([P, LANES, P], F32, name="bank", tag="sums")
        for lane in range(LANES):
            nc.tensor.transpose(bank[:, lane, :], abs_row[:, lane * P : (lane + 1) * P], ident[:])
        abs_ts = keep.tile([P, LANES], F32, name="abs_ts")
        nc.scalar.activation(abs_ts[:], bank[:, :, 0], COPY)
        neg_square = keep.tile([P, LANES], F32, name="neg_square")
        nc.vector.scalar_tensor_tensor(neg_square[:], abs_ts[:], -1.0, abs_ts[:], MULT, MULT)

        k_f32 = keep.tile([P, LANES, N], F32, name="k_f32")
        kn_in = keep.tile([P, LANES, P * LANES], BF16, name="kn_in", align_bytes=64)
        kn_codes = keep.tile([P, D], U32, name="kn_codes", align_bytes=64)
        kn_scales = keep.tile([P, D], U8, name="kn_scales", align_bytes=64)
        kd_in = keep.tile([P, N * LANES], BF16, name="kd_in", align_bytes=64)
        kd_codes = keep.tile([P, N], U32, name="kd_codes", align_bytes=64)
        kd_scales = keep.tile([P, N], U8, name="kd_scales", align_bytes=64)

        def gather(t):
            nc.vector.tensor_tensor(k_f32[:, t, :], books[t][:].indirect(offsets[:]), norm_row[:], MULT)

        def turn_k(t):
            pairs = ring.tile([P, N], BF16, name="pairs", tag="pairs", align_bytes=64)
            nc.scalar.copy(
                pairs[:].rearrange("p (u f i e) -> p u f e i", u=2, i=BLOCK_PARTITIONS, e=2),
                k_f32[:, t, :].rearrange("p (f u e i) -> p u f e i", u=2, i=BLOCK_PARTITIONS, e=2),
            )
            words = pairs[:].bitcast(F32)
            turned = psum.tile([P, LANES, P], F32, name="bank", tag="sums")
            for u in range(2):
                nc.tensor.transpose(turned[:, u, :], words[:, u * P : (u + 1) * P], ident[:])
            nc.scalar.copy(
                kn_in[:, t, :].bitcast(F32).rearrange("n (p u) -> n p u", u=2),
                turned[:, 0:2, :].rearrange("n u p -> n p u"),
            )
            cols = slice(t * P, (t + 1) * P)
            nc.vector.quantize_mx(kn_codes[:, cols].bitcast(E4M3), kn_scales[:, cols], kn_in[:, t, :])

        x_in = [keep.tile([P, PASS * LANES], BF16, name="x_in%d" % g, align_bytes=64) for g in range(GROUPS)]
        x_codes = [keep.tile([P, PASS], U32, name="x_codes%d" % g, align_bytes=64) for g in range(GROUPS)]
        x_scales = [keep.tile([P, PASS], U8, name="x_scales%d" % g, align_bytes=64) for g in range(GROUPS)]

        def weave_x(g):
            dealt = x_in[g][:].rearrange("p (t m j) -> p m j t", t=LANES, j=LANES)
            for a in range(2):
                nc.scalar.copy(
                    dealt[:, a * (P // 2) : (a + 1) * (P // 2), :, :],
                    x_raw[2 * g + a][:].rearrange("p j (m t) -> p m j t", t=LANES),
                )

        def quantize_x(g):
            width = P if g == 0 else PASS
            for c in range(0, PASS, width):
                nc.vector.quantize_mx(
                    x_codes[g][:, c : c + width].bitcast(E4M3),
                    x_scales[g][:, c : c + width],
                    x_in[g][:, c * LANES : (c + width) * LANES],
                )

        for t in range(LANES):
            gather(t)
            if t < LANES - 1:
                turn_k(t)
        nc.vector.tensor_copy(
            kd_in[:].rearrange("p (c i t) -> p c t i", i=4, t=LANES),
            k_f32[:].rearrange("p t (c i) -> p c t i", i=4),
        )
        nc.vector.quantize_mx(kd_codes[:].bitcast(E4M3), kd_scales[:], kd_in[:])
        weave_x(0)
        quantize_x(0)

        result = [keep.tile([P, LANES, D], F32, name="result%d" % g) for g in range(GROUPS)]
        out_rows = out_0.rearrange("(g m t) d -> g m t d", g=GROUPS, t=LANES)
        plane_scales = keep.tile([P, GROUPS, D], U8, name="plane_scales", align_bytes=64)
        shared = [keep.tile([P, N], F32, name="shared%d" % b, align_bytes=64) for b in range(SHARED)]
        scores = {}
        margin = {}
        weighted_turned = {}
        slack = {}
        h_in = {}

        def by_lanes(ap):
            return ap.rearrange("m (l f i) -> m f l i", l=LANES, i=BLOCK_PARTITIONS)

        def as_loaded(ap):
            return ap.rearrange("m (f l i) -> m f l i", l=LANES, i=BLOCK_PARTITIONS)

        def turn(src, tag):
            turned = psum.tile([P, LANES, P], F32, name=tag, tag=tag)
            for lane in range(LANES):
                nc.tensor.transpose(turned[:, lane, :], src[:, lane * P : (lane + 1) * P], ident[:])
            return turned

        def weigh(i):
            g, t = divmod(i, LANES)
            nc.gpsimd.tensor_scalar(
                by_lanes(shared[i % SHARED][:]), as_loaded(y_raw[i][:]), wt_col[:, g, t : t + 1], -1.0, MULT, MULT
            )

        def score(i):
            g, t = divmod(i, LANES)
            cols = slice(t * P, (t + 1) * P)
            scores[i] = psum.tile([P, N], F32, name="scores", tag="scores")
            for repeat in range(2 if i in REPEATED else 1):
                nc.tensor.matmul_mx(
                    scores[i][:], x_codes[g][:, cols].bitcast(E4M3), x_scales[g][:, cols],
                    kd_codes[:].bitcast(E4M3), kd_scales[:], start=True, stop=True,
                )

        def sign(i):
            margin[i] = ring.tile([P, N], F32, name="margin", tag="margin")
            nc.vector.tensor_tensor(by_lanes(margin[i][:]), as_loaded(scores[i][:]), as_loaded(y_raw[i][:]), MULT)

        def hinge(i):
            turned = turn(margin[i], "margin_turned")
            slack[i] = ring.tile([P, LANES, P], F32, name="slack", tag="slack")
            for lane in range(LANES):
                nc.scalar.activation(
                    slack[i][:, lane, :], turned[:, lane, :], RELU,
                    bias=abs_ts[:, lane : lane + 1], scale=neg_square[:, lane : lane + 1],
                )

        def turn_weighted(i):
            weighted_turned[i] = turn(shared[i % SHARED], "weighted_turned")

        def gradient(i):
            h_in[i] = shared[i % SHARED][:, 0 : N // 2].bitcast(BF16)
            nc.vector.tensor_tensor(
                h_in[i].rearrange("n (c e l) -> n c l e", e=2, l=LANES),
                weighted_turned[i][:].rearrange("n l (c e) -> n c l e", e=2),
                slack[i][:].rearrange("n l (c e) -> n c l e", e=2),
                MULT,
            )

        def back(i):
            g, t = divmod(i, LANES)
            h_codes = ring.tile([P, P], U32, name="h_codes", tag="h_codes", align_bytes=64)
            h_scales = ring.tile([P, P], U8, name="h_scales", tag="h_scales", align_bytes=64)
            nc.vector.quantize_mx(h_codes[:].bitcast(E5M2), h_scales[:], h_in[i])
            if i + SHARED < TILES:
                weigh(i + SHARED)
            sums = psum.tile([P, D], F32, name="sums", tag="sums")
            nc.tensor.matmul_mx(
                sums[:], h_codes[:].bitcast(E5M2), h_scales[:],
                kn_codes[:].bitcast(E4M3), kn_scales[:], start=True, stop=True,
            )
            dst = result[g][:, t, :].rearrange("m (p j) -> m p j", j=LANES)
            src = sums[:].rearrange("m (j p) -> m p j", j=LANES)
            width = P // 2 if i == TILES - 1 else P
            copy = nc.vector.tensor_copy if g == GROUPS - 1 and t % 2 == 0 else nc.scalar.copy
            for c in range(0, P, width):
                copy(dst[:, c : c + width, :], src[:, c : c + width, :])
            nc.sync.dma_start(out_rows[g, :, t, :], result[g][:, t, :])

        def planes(g):
            last = g == GROUPS - 1
            words_out = out_1[g].rearrange("p d l -> p (d l)").bitcast(I32)
            woven = []
            for a in range(2):
                cols = slice(a * HALF, (a + 1) * HALF)
                half = keep.tile([P, HALF * LANES], BF16, name="woven%d_%d" % (g, a), align_bytes=64)
                copy = nc.vector.tensor_copy if last and a == 1 else nc.scalar.copy
                copy(
                    half[:].rearrange("p (c i t) -> p c t i", i=4, t=LANES),
                    result[g][:, :, cols].rearrange("p t (c i) -> p c t i", i=4),
                )
                woven.append(half)
            for a in (1, 0) if last else (0, 1):
                cols = slice(a * HALF, (a + 1) * HALF)
                codes = keep.tile([P, HALF], U32, name="plane_codes%d_%d" % (g, a), align_bytes=64)
                nc.vector.quantize_mx(codes[:].bitcast(E4M3), plane_scales[:, g, cols], woven[a][:])
                nc.sync.dma_start(words_out[:, cols], codes[:].bitcast(I32))

        for i in range(SHARED):
            weigh(i)
        stages = [(sign, 1), (score, 0), (hinge, 1), (gradient, 4), (turn_weighted, 2), (back, 4)]
        depth = max(delay for stage, delay in stages)
        for step in range(TILES + depth):
            if step == depth - 2:
                turn_k(LANES - 1)
            for stage, delay in stages:
                if 0 <= step - delay < TILES:
                    stage(step - delay)
            if step == LANES - 1:
                weave_x(1)
                quantize_x(1)
        for g in range(GROUPS):
            planes(g)

        scales_out = out_2.bitcast(I32).rearrange("g f d -> f g d")
        scale_words = plane_scales[:].bitcast(I32)
        for q in range(4):
            queue = nc.scalar if q % 2 else nc.sync
            queue.dma_start(scales_out[4 * q : 4 * q + 4, :, :], scale_words[32 * q : 32 * q + 4, :, :])
